import numpy as np
import ml_dtypes


def mxq(x, axis, fmt="e4m3"):
    dtype, down = {"e4m3": (ml_dtypes.float8_e4m3fn, 7), "e5m2": (ml_dtypes.float8_e5m2, 14)}[fmt]
    v = np.moveaxis(np.asarray(x, np.float32).astype(ml_dtypes.bfloat16).astype(np.float64), axis, -1)
    blocks = v.reshape(v.shape[:-1] + (-1, 32))
    amax = np.abs(blocks).max(-1, keepdims=True)
    byte = np.maximum(np.where(amax > 0, np.frexp(amax)[1] - 1 + 127, 0) - down, 1)
    scale = np.exp2(byte - 127.0)
    codes = (blocks / scale).astype(np.float32).astype(dtype).astype(np.float64)
    return np.moveaxis((codes * scale).reshape(v.shape), -1, axis)


WIDE = False


def mx_kscale(k):
    if not WIDE:
        return np.ones(k)
    levels = np.array([10, -10, 5, -5, 0])
    if k % 512:
        return np.exp2(np.random.permutation(np.resize(levels, k // 32))).repeat(32)
    a = np.empty((k // 512, 16))
    for p in range(k // 512):
        a[p, :8] = np.random.permutation(np.resize(levels, 8))
        for g in range(8):
            far = levels[np.abs(levels - a[p, g]) >= 10]
            a[p, g + 8] = far[np.random.randint(len(far))]
    return np.exp2(a.ravel()).repeat(32)


def f64(x):
    return np.asarray(x).astype(np.float64)


def striped(idx):
    return np.tile(idx.reshape(-1, 16).T, (8, 1)).astype(np.uint16)


def unstriped(offs):
    return offs[:16].T.reshape(-1).astype(np.int64)


E2M1 = np.array([0.0, 0.5, 1.0, 1.5, 2.0, 3.0, 4.0, 6.0, -0.0, -0.5, -1.0, -1.5, -2.0, -3.0, -4.0, -6.0])


def pack_weight(w, fmt):
    k, n = w.shape
    w = f64(np.asarray(w, np.float32).astype(ml_dtypes.bfloat16)).reshape(k // 32, 32, n)
    amax = np.abs(w).max(1)
    if fmt == "e4m3":
        byte = np.frexp(amax)[1] - 1 + 127 - 7
    else:
        mant, ex = np.frexp(amax / 6.0)
        byte = np.where(mant > 0.5, ex, ex - 1) + 127
    byte = np.clip(np.where(amax > 0, byte, 1), 1, 254)
    scaled = (w * np.exp2(127.0 - byte)[:, None, :]).reshape(k, n).astype(np.float32)
    by_word = np.ascontiguousarray(scaled.reshape(k // 512, 128, 4, n).transpose(0, 1, 3, 2))
    if fmt == "e4m3":
        words = by_word.astype(ml_dtypes.float8_e4m3fn).view(np.uint8)
    else:
        c = by_word.astype(ml_dtypes.float4_e2m1fn).view(np.uint8) & 0xF
        words = (c[..., 0::2] | (c[..., 1::2] << 4)).reshape(k // 512, 128, 2 * n)
    return np.ascontiguousarray(words), np.ascontiguousarray(byte.astype(np.uint8).reshape(k // 512, 16, n))


def unpack_weight(words, scales, fmt):
    g, _, n = scales.shape
    words = np.ascontiguousarray(words).reshape(g, 128, n, -1)
    if fmt == "e4m3":
        vals = words.view(ml_dtypes.float8_e4m3fn).astype(np.float64)
    else:
        nib = np.empty((g, 128, n, 4), np.uint8)
        nib[..., 0::2] = words & 0xF
        nib[..., 1::2] = words >> 4
        vals = E2M1[nib]
    vals = vals * np.repeat(np.exp2(scales.astype(np.float64) - 127.0), 8, axis=1)[..., None]
    return vals.transpose(0, 1, 3, 2).reshape(g * 512, n)


def gelu(v):
    return 0.5 * v * (1.0 + np.tanh(np.sqrt(2.0 / np.pi) * (v + 0.044715 * v**3)))


def striped8(idx):
    return np.concatenate([v.reshape(-1, 16).T for v in idx]).astype(np.uint16)


def unstriped8(offs):
    return np.stack([offs[16 * g:16 * g + 16].T.reshape(-1) for g in range(8)]).astype(np.int64)


def heads(h, wgt, idx8):
    r = np.arange(h.shape[0])
    return wgt[r // 4 % 128] * h[r[:, None], idx8[r % 512 // 64]]


def put_heads(h, wgs, idx8, t2):
    r = np.arange(h.shape[0])
    page = np.zeros((h.shape[0], t2))
    page[r[:, None], idx8[r % 512 // 64]] = wgs[r // 4 % 128] * h
    return page


K, T, H, S, P, T2, N = 512, 4096, 1024, 1024, 1024, 2048, 384

def setup_inputs():
    n = np.random.standard_normal
    s = mx_kscale(K)[:, None]
    u = mx_kscale(H)[:, None]
    d = {}
    d["tab_words"], d["tab_scales"] = pack_weight(n((K, T)) * s, "e4m3")
    d["offs"] = striped(np.random.permutation(T)[:S])
    d["offs2"] = striped8(np.stack([np.random.permutation(T2)[:S] for _ in range(8)]))
    d["offs3"] = striped8(np.stack([np.random.permutation(T2)[:P] for _ in range(8)]))
    d["wt_words"], d["wt_scales"] = pack_weight(1.5 * n((K, H)) / K**0.5 / s, "e2m1")
    d["bt"] = (0.6 * n(H)).astype(np.float32)
    d["gain"] = (1.2 * np.exp(0.3 * n(H)) * u[:, 0]).astype(np.float32)
    d["ws"] = (0.8 * n((K, H)) / K**0.5 / s * u.T).astype(np.float32)
    d["wgs"] = np.repeat(np.random.uniform(0.5, 2.0, (8, S)), 16, axis=0).astype(np.float32)
    d["wgt"] = np.repeat(np.random.uniform(0.5, 2.0, (8, P)), 16, axis=0).astype(np.float32)
    d["bellows"] = (n((H, P)) * u).astype(np.float32)
    d["wo"] = (n((H, N)) / H**0.5 / u).astype(np.float32)
    d["bo"] = (0.6 * n(N)).astype(np.float32)
    return d

def reference(tab_words, tab_scales, offs, offs2, offs3, wt_words, wt_scales, bt, gain, ws, wgs, wgt, bellows, wo, bo):
    v = unpack_weight(tab_words, tab_scales, "e4m3")[:, unstriped(offs)]
    wt = unpack_weight(wt_words, wt_scales, "e2m1")
    bend = np.tanh((wt.T @ v) + f64(bt)[:, None])
    straight = mxq(f64(ws), 0, "e4m3").T @ v
    h = f64(gain)[:, None] * bend + straight
    page = put_heads(h, f64(wgs), unstriped8(offs2), T2)
    x = heads(page, f64(wgt), unstriped8(offs3))
    z = x + f64(bellows)
    y = mxq(f64(wo), 0, "e4m3").T @ mxq(z, 0, "e4m3")
    return y + f64(bo)[:, None]

@@ -1,0 +1,362 @@
+from contextlib import ExitStack
+
+import concourse.mybir as mybir
+from concourse.masks import make_identity
+
+K, T, H, S, PICKS, T2, N = 512, 4096, 1024, 1024, 1024, 2048, 384
+FLOPS = 2 * (2 * K * H * S + H * N * PICKS)
+
+F32 = mybir.dt.float32
+BF16 = mybir.dt.bfloat16
+I32 = mybir.dt.int32
+U32 = mybir.dt.uint32
+U16 = mybir.dt.uint16
+U8 = mybir.dt.uint8
+FP8X4 = mybir.dt.float8_e4m3fn_x4
+FP4X4 = mybir.dt.float4_e2m1fn_x4
+MULT = mybir.AluOpType.mult
+ADD = mybir.AluOpType.add
+ACT = mybir.ActivationFunctionType
+
+P = 128
+HALF = 512
+QUARTER = 256
+SLICES = 8
+VECTOR_SLICES = 2
+PAGES = 3
+H_TILES = 4
+STAGE_TILES = 3
+LANDING = 112
+
+
+def tile_list_reed_register_response_kernel(
+    tc, tab_words, tab_scales, offs, offs2, offs3, wt_words, wt_scales, bt, gain, ws, wgs, wgt, bellows, wo, bo, out
+):
+    nc = tc.nc
+    with ExitStack() as ctx:
+        keep = ctx.enter_context(tc.tile_pool(name="keep", bufs=1))
+        psum = ctx.enter_context(tc.psum_pool(name="psum", bufs=1))
+
+        def sb(name, width, dtype):
+            return keep.tile([P, width], dtype, name=name, align_bytes=64)
+
+        banks = [psum.tile([P, HALF], F32, name="bank%d" % n) for n in range(8)]
+        turn = [0]
+
+        def next_bank():
+            bank = banks[turn[0] % 8]
+            turn[0] = turn[0] + 1
+            return bank
+
+        def cols(n, width):
+            return slice(n * width, (n + 1) * width)
+
+        list1 = keep.tile([P, S // 16], U16, name="list1")
+        list2 = keep.tile([P, S // 16], U16, name="list2")
+        list3 = keep.tile([P, PICKS // 16], U16, name="list3")
+        bt_sb = sb("bt_sb", SLICES, F32)
+        gain_sb = sb("gain_sb", SLICES, F32)
+        bo_sb = sb("bo_sb", 3, F32)
+        ident = sb("ident", P, F32)
+        table = sb("table", T, I32)
+        table_sc = sb("table_sc", T, U8)
+        v_codes = sb("v_codes", S, U32)
+        picked_sc = sb("picked_sc", S, U8)
+        planes = sb("planes", S + H, U8)
+        v_sc = planes[:, 0:S]
+        wt_sc = planes[:, S : S + H]
+        wt_raw = sb("wt_raw", 2 * H, U8)
+        wt_codes = sb("wt_codes", 2 * H, U8)
+        wt_sc_raw = sb("wt_sc_raw", H, U8)
+        stage_a = sb("stage_a", 4 * HALF, F32)
+        stage_b = sb("stage_b", 4 * HALF, F32)
+        stage_c = sb("stage_c", 2 * HALF, F32)
+        stage_d = sb("stage_d", 8 * N, F32)
+        ws_codes = sb("ws_codes", H, U32)
+        ws_sc = sb("ws_sc", H, U8)
+        wo_bf = sb("wo_bf", 8 * N, BF16)
+        wo_codes = sb("wo_codes", 2 * N, U32)
+        wo_sc = sb("wo_sc", 2 * N, U8)
+        pages = [sb("page%d" % n, T2, F32) for n in range(PAGES)]
+        h_sb = [sb("h%d" % n, S, F32) for n in range(H_TILES)]
+        gained = {s: sb("gained%d" % s, S, F32) for s in range(VECTOR_SLICES, SLICES)}
+        turned = {s: sb("turned%d" % s, S, F32) for s in range(VECTOR_SLICES, SLICES)}
+        bend_st = [sb("bend%d" % n, HALF, F32) for n in range(STAGE_TILES)]
+        straight_st = [sb("straight%d" % n, HALF, F32) for n in range(STAGE_TILES)]
+        z_turned = [[sb("zt%d_%d" % (u, q), HALF, BF16) for q in range(4)] for u in range(2)]
+        z0 = sb("z0", 4 * PICKS, BF16)
+        z0_codes = sb("z0_codes", PICKS, U32)
+        z0_sc = sb("z0_sc", PICKS, U8)
+        z1 = [sb("z1_%d" % q, 3 * QUARTER, F32) for q in range(4)]
+        z1_codes = [sb("z1_codes%d" % q, QUARTER, U32) for q in range(4)]
+        z1_sc = [sb("z1_sc%d" % q, QUARTER, U8) for q in range(4)]
+
+        wgs_sb = stage_a[:, 0:S]
+        wgt_sb = stage_a[:, S : 2 * S]
+        x_sb = {s: turned[s + 2][:] for s in range(SLICES - 2)}
+        x_sb[6] = x_sb[4]
+        x_sb[7] = x_sb[5]
+        bel_sb = {s: gained[s][:] for s in gained}
+        bel_sb[0] = stage_b[:, 0:PICKS]
+        bel_sb[1] = stage_b[:, PICKS : 2 * PICKS]
+        bel_rows = bellows.rearrange("(b p i) m -> b i p m", b=2, i=4)
+        ws_rows = ws.rearrange("(p j) c -> p j c", j=4)
+
+        nc.sync.dma_start(list1[:], offs)
+        nc.sync.dma_start(table_sc[LANDING:P, :].bitcast(I32), tab_scales[0].bitcast(I32))
+        nc.sync.dma_start(wt_sc_raw[LANDING:P, :].bitcast(I32), wt_scales[0].bitcast(I32))
+        nc.sync.dma_start(wt_raw[:].bitcast(I32), wt_words[0].bitcast(I32))
+        nc.sync.dma_start(list2[:], offs2)
+        nc.sync.dma_start(list3[:], offs3)
+        nc.sync.dma_start(stage_a[:].rearrange("p (j c) -> p j c", j=4), ws_rows[:, :, cols(0, HALF)])
+        nc.sync.dma_start(table[:], tab_words[0].rearrange("p t i -> p (t i)").bitcast(I32))
+        nc.gpsimd.dma_start(bt_sb[:].rearrange("p (b i) -> p b i", b=2), bt.rearrange("(b p i) -> p b i", b=2, i=4))
+        nc.gpsimd.dma_start(gain_sb[:].rearrange("p (b i) -> p b i", b=2), gain.rearrange("(b p i) -> p b i", b=2, i=4))
+        with nc.allow_non_contiguous_dma(reason="one bias value for each partition"):
+            nc.gpsimd.dma_start(bo_sb[:], bo.rearrange("(t p) -> p t", p=P))
+        make_identity(nc, ident[:])
+        nc.vector.memset(table_sc[0:LANDING, :].bitcast(I32), 0)
+        nc.vector.memset(wt_sc_raw[0:LANDING, :].bitcast(I32), 0)
+
+        nc.vector.tensor_copy(picked_sc[:], table_sc[:].indirect(list1[:]))
+        nc.vector.tensor_copy(v_sc.bitcast(I32), picked_sc[:].bitcast(I32))
+        nc.vector.tensor_copy(
+            wt_sc.rearrange("p (b i q) -> p b i q", b=2, i=4),
+            wt_sc_raw[:].rearrange("p (b q i) -> p b i q", b=2, i=4),
+        )
+        for quad in range(4):
+            nc.sync.dma_start(
+                planes[32 * quad : 32 * quad + 4, :].bitcast(I32),
+                planes[LANDING + 4 * quad : LANDING + 4 * quad + 4, :].bitcast(I32),
+            )
+        nc.vector.tensor_copy(
+            wt_codes[:].rearrange("p (b i q e) -> p b i q e", b=2, i=4, e=2),
+            wt_raw[:].rearrange("p (b q i e) -> p b i q e", b=2, i=4, e=2),
+        )
+        for page in pages:
+            engine = nc.vector if page is pages[0] else nc.gpsimd
+            for n in range(4):
+                engine.memset(page[:, cols(n, HALF)], 0.0)
+
+        def quantize_ws(b, raw, rounded):
+            nc.scalar.copy(
+                rounded.rearrange("p (t m j) -> p m j t", t=4, j=4),
+                raw.rearrange("p (j m t) -> p m j t", j=4, t=4),
+            )
+            nc.vector.quantize_mx(ws_codes[:, cols(b, HALF)].bitcast(FP8X4), ws_sc[:, cols(b, HALF)], rounded)
+
+        quantize_ws(0, stage_a[:], stage_b[:, 0 : 2 * HALF].bitcast(BF16))
+        nc.sync.dma_start(wgs_sb, wgs)
+        nc.sync.dma_start(wgt_sb, wgt)
+        nc.sync.dma_start(stage_b[:].rearrange("p (j c) -> p j c", j=4), ws_rows[:, :, cols(1, HALF)])
+
+        for half in range(2):
+            nc.vector.tensor_copy(v_codes[:, cols(half, HALF)], table[:].bitcast(U32).indirect(list1[:, cols(half, 32)]))
+
+        def products(s, half):
+            j = cols(half, HALF)
+            curved, straight = next_bank(), next_bank()
+            nc.tensor.matmul_mx(
+                curved[:],
+                lhsT=wt_codes[:, cols(s, 2 * P)].bitcast(FP4X4),
+                lhsT_scale=wt_sc[:, cols(s, P)],
+                rhs=v_codes[:, j].bitcast(FP8X4),
+                rhs_scale=v_sc[:, j],
+                start=True,
+                stop=True,
+            )
+            nc.tensor.matmul_mx(
+                straight[:],
+                lhsT=ws_codes[:, cols(s, P)].bitcast(FP8X4),
+                lhsT_scale=ws_sc[:, cols(s, P)],
+                rhs=v_codes[:, j].bitcast(FP8X4),
+                rhs_scale=v_sc[:, j],
+                start=True,
+                stop=True,
+            )
+            return curved, straight
+
+        def add_turned(bank, parts):
+            for n, (columns, block) in enumerate(parts):
+                nc.tensor.matmul(
+                    bank[:, columns], lhsT=block, rhs=ident[:], is_transpose=True, start=(n == 0), stop=(n == len(parts) - 1)
+                )
+
+        def h_on_vector(s, half):
+            curved, straight = products(s, half)
+            bend = stage_d[:, s * S + half * HALF : s * S + (half + 1) * HALF]
+            nc.scalar.activation(bend, curved[:], ACT.Tanh, bias=bt_sb[:, s : s + 1])
+            nc.vector.scalar_tensor_tensor(
+                h_sb[s % H_TILES][:, cols(half, HALF)], bend, gain_sb[:, s : s + 1], straight[:], MULT, ADD
+            )
+
+        def h_front(n):
+            s, half = divmod(n, 2)
+            curved, straight = products(s, half)
+            bend = bend_st[n % STAGE_TILES]
+            nc.scalar.activation(bend[:], curved[:], ACT.Tanh, bias=bt_sb[:, s : s + 1])
+            nc.scalar.copy(straight_st[n % STAGE_TILES][:], straight[:])
+            nc.scalar.activation(gained[s][:, cols(half, HALF)], bend[:], ACT.Copy, scale=gain_sb[:, s : s + 1])
+
+        def h_middle(n):
+            s, half = divmod(n, 2)
+            bank = next_bank()
+            parts = [(cols(a, P), straight_st[n % STAGE_TILES][:, cols(a, P)]) for a in range(4)]
+            parts = parts + [(cols(a, P), gained[s][:, cols(4 * half + a, P)]) for a in range(4)]
+            add_turned(bank, parts)
+            nc.scalar.copy(turned[s][:, cols(half, HALF)], bank[:])
+
+        def h_back(n):
+            s, half = divmod(n, 2)
+            bank = next_bank()
+            for a in range(4):
+                nc.tensor.transpose(bank[:, cols(a, P)], turned[s][:, cols(4 * half + a, P)], ident[:])
+            nc.scalar.copy(h_sb[s % H_TILES][:, cols(half, HALF)], bank[:])
+
+        def scatter(s, piece, pieces):
+            width = S // pieces
+            nc.vector.tensor_tensor(
+                pages[s % PAGES][:].indirect(list2[:, cols(piece, width // 16)]),
+                h_sb[s % H_TILES][:, cols(piece, width)],
+                wgs_sb[:, cols(piece, width)],
+                MULT,
+            )
+
+        def gather(s, piece, pieces):
+            width = PICKS // pieces
+            nc.vector.tensor_tensor(
+                x_sb[s][:, cols(piece, width)],
+                pages[s % PAGES][:].indirect(list3[:, cols(piece, width // 16)]),
+                wgt_sb[:, cols(piece, width)],
+                MULT,
+            )
+
+        def load_bellows(s):
+            nc.sync.dma_start(bel_sb[s], bel_rows[s // 4, s % 4])
+
+        h_on_vector(0, 0)
+        scatter(0, 0, 2)
+        h_on_vector(0, 1)
+        h_on_vector(1, 0)
+        scatter(0, 1, 2)
+        h_on_vector(1, 1)
+        scatter(1, 0, 1)
+        quantize_ws(1, stage_b[:], stage_c[:].bitcast(BF16))
+        load_bellows(0)
+        load_bellows(1)
+        nc.sync.dma_start(
+            stage_d[:].rearrange("p (b x) -> p b x", b=2), wo.rearrange("(b p i) n -> p b (i n)", b=2, i=4)
+        )
+
+        first, last = 2 * VECTOR_SLICES, 2 * SLICES - 1
+        h_front(first)
+        for n in range(first, last + 2):
+            if n + 1 <= last:
+                h_front(n + 1)
+            if n <= last:
+                h_middle(n)
+                if n % 2 == 1:
+                    load_bellows(n // 2)
+            if n - 1 >= first:
+                h_back(n - 1)
+                if (n - 1) % 2 == 1:
+                    s = (n - 1) // 2
+                    gather(s - 2, 0, 1)
+                    scatter(s, 0, 1)
+
+        for b in range(2):
+            nc.scalar.copy(
+                wo_bf[:, cols(b, 4 * N)].rearrange("p (c k i) -> p c i k", k=4, i=4),
+                stage_d[:, cols(b, 4 * N)].rearrange("p (i c k) -> p c i k", i=4, k=4),
+            )
+        for lo, hi in ((0, 512), (512, 768)):
+            nc.vector.quantize_mx(wo_codes[:, lo:hi].bitcast(FP8X4), wo_sc[:, lo:hi], wo_bf[:, 4 * lo : 4 * hi])
+
+        def z_parts(source, s, q):
+            e = s % 2
+            return [(cols(2 * a + e, P), source[s][:, cols(2 * q + a, P)]) for a in range(2)]
+
+        def z_round(bank, rounded):
+            nc.scalar.copy(
+                rounded[:].rearrange("m (a p e) -> m a p e", a=2, e=2),
+                bank[:].rearrange("m (a e p) -> m a p e", a=2, e=2),
+            )
+
+        def z_pair(pair, q):
+            bank = next_bank()
+            s0, s1 = 2 * pair, 2 * pair + 1
+            add_turned(bank, z_parts(bel_sb, s0, q) + z_parts(bel_sb, s1, q) + z_parts(x_sb, s1, q) + z_parts(x_sb, s0, q))
+            z_round(bank, z_turned[pair % 2][q])
+
+        def z_words(bank, u, rounded):
+            for a in range(2):
+                nc.tensor.transpose(bank[:, cols(2 * u + a, P)], rounded[:].bitcast(F32)[:, cols(a, P)], ident[:])
+
+        def z_weave(z_quarter, bank):
+            nc.scalar.copy(
+                z_quarter.bitcast(F32).rearrange("p (m u) -> p m u", u=2), bank[:].rearrange("p (u m) -> p m u", u=2)
+            )
+
+        for pair in range(2):
+            for q in range(4):
+                z_pair(pair, q)
+        for q in range(4):
+            bank = next_bank()
+            z_words(bank, 0, z_turned[0][q])
+            z_words(bank, 1, z_turned[1][q])
+            z_weave(z0[:, cols(q, 4 * QUARTER)], bank)
+        nc.vector.quantize_mx(z0_codes[:].bitcast(FP8X4), z0_sc[:], z0[:])
+        for q in range(4):
+            z_pair(2, q)
+        word_banks = [next_bank() for q in range(4)]
+        for q in range(4):
+            z_words(word_banks[q], 0, z_turned[0][q])
+
+        def closing(target, t, b, q, start, stop):
+            codes = z0_codes[:, cols(q, QUARTER)] if b == 0 else z1_codes[q][:]
+            scales = z0_sc[:, cols(q, QUARTER)] if b == 0 else z1_sc[q][:]
+            n = cols(3 * b + t, P)
+            nc.tensor.matmul_mx(
+                target,
+                lhsT=wo_codes[:, n].bitcast(FP8X4),
+                lhsT_scale=wo_sc[:, n],
+                rhs=codes.bitcast(FP8X4),
+                rhs_scale=scales,
+                start=start,
+                stop=stop,
+            )
+
+        sum_banks = [next_bank() for q in range(4)]
+        for q in range(4):
+            gather(6, q, 4)
+            gather(7, q, 4)
+            add_turned(sum_banks[q], z_parts(bel_sb, 6, q) + z_parts(bel_sb, 7, q) + z_parts(x_sb, 6, q) + z_parts(x_sb, 7, q))
+        out_rows = out.rearrange("(t p) m -> p t m", p=P)
+
+        def z_close(q):
+            two, one = sum_banks[q], word_banks[q]
+            z_quarter = z1[q][:, 0 : 2 * QUARTER].bitcast(BF16)
+            z_round(two, z_turned[1][q % 2])
+            z_words(one, 1, z_turned[1][q % 2])
+            for t in range(2):
+                closing(two[:, cols(t, QUARTER)], t, 0, q, t == 0, False)
+            z_weave(z_quarter, one)
+            closing(one[:, 0:QUARTER], 2, 0, q, True, False)
+            nc.vector.quantize_mx(z1_codes[q][:].bitcast(FP8X4), z1_sc[q][:], z_quarter)
+            for t in range(2):
+                closing(two[:, cols(t, QUARTER)], t, 1, q, False, t == 1)
+            closing(one[:, 0:QUARTER], 2, 1, q, False, True)
+
+        def store(q):
+            two, one = sum_banks[q], word_banks[q]
+            y = z1[(q + 1) % 4]
+            for t in range(2):
+                nc.vector.tensor_scalar(y[:, cols(t, QUARTER)], two[:, cols(t, QUARTER)], bo_sb[:, t : t + 1], None, ADD)
+            nc.scalar.activation(y[:, cols(2, QUARTER)], one[:, 0:QUARTER], ACT.Identity, bias=bo_sb[:, 2:3])
+            nc.sync.dma_start(out_rows[:, :, cols(q, QUARTER)], y[:].rearrange("p (t m) -> p t m", t=3))
+
+        z_close(0)
+        for q in range(4):
+            if q + 1 < 4:
+                z_close(q + 1)
+            store(q)

@@ -79,8 +79,10 @@ def tile_list_reed_register_response_kernel(
         wo_sc = sb("wo_sc", 2 * N, U8)
         pages = [sb("page%d" % n, T2, F32) for n in range(PAGES)]
         h_sb = [sb("h%d" % n, S, F32) for n in range(H_TILES)]
-        gained = {s: sb("gained%d" % s, S, F32) for s in range(VECTOR_SLICES, SLICES)}
-        turned = {s: sb("turned%d" % s, S, F32) for s in range(VECTOR_SLICES, SLICES)}
+        gained_all = sb("gained_all", (SLICES - VECTOR_SLICES) * S, F32)
+        gained = {s: gained_all[:, cols(s - VECTOR_SLICES, S)] for s in range(VECTOR_SLICES, SLICES)}
+        turned_all = sb("turned_all", (SLICES - VECTOR_SLICES) * S, F32)
+        turned = {s: turned_all[:, cols(s - VECTOR_SLICES, S)] for s in range(VECTOR_SLICES, SLICES)}
         bend_st = [sb("bend%d" % n, HALF, F32) for n in range(STAGE_TILES)]
         straight_st = [sb("straight%d" % n, HALF, F32) for n in range(STAGE_TILES)]
         z_turned = [[sb("zt%d_%d" % (u, q), HALF, BF16) for q in range(4)] for u in range(2)]
@@ -93,12 +95,14 @@ def tile_list_reed_register_response_kernel(
 
         wgs_sb = stage_a[:, 0:S]
         wgt_sb = stage_a[:, S : 2 * S]
-        x_sb = {s: turned[s + 2][:] for s in range(SLICES - 2)}
+        x_sb = {s: turned[s + 2] for s in range(SLICES - 2)}
         x_sb[6] = x_sb[4]
         x_sb[7] = x_sb[5]
-        bel_sb = {s: gained[s][:] for s in gained}
+        x_q = {(s, q): x_sb[s][:, cols(q, QUARTER)] for s in range(SLICES) for q in range(4)}
+        bel_sb = dict(gained)
         bel_sb[0] = stage_b[:, 0:PICKS]
         bel_sb[1] = stage_b[:, PICKS : 2 * PICKS]
+        bel_q = {(s, q): bel_sb[s][:, cols(q, QUARTER)] for s in range(SLICES) for q in range(4)}
         bel_rows = bellows.rearrange("(b p i) m -> b i p m", b=2, i=4)
         ws_rows = ws.rearrange("(p j) c -> p j c", j=4)
 
@@ -140,8 +144,8 @@ def tile_list_reed_register_response_kernel(
 
         def quantize_ws(b, raw, rounded):
             nc.scalar.copy(
-                rounded.rearrange("p (t m j) -> p m j t", t=4, j=4),
-                raw.rearrange("p (j m t) -> p m j t", j=4, t=4),
+                rounded.rearrange("p (t m j) -> p m t j", t=4, j=4),
+                raw.rearrange("p (j m t) -> p m t j", j=4, t=4),
             )
             nc.vector.quantize_mx(ws_codes[:, cols(b, HALF)].bitcast(FP8X4), ws_sc[:, cols(b, HALF)], rounded)
 
@@ -176,11 +180,11 @@ def tile_list_reed_register_response_kernel(
             )
             return curved, straight
 
-        def add_turned(bank, parts):
+        def add_turned(bank, parts, opens=True, closes=True):
             for n, (columns, block) in enumerate(parts):
-                nc.tensor.matmul(
-                    bank[:, columns], lhsT=block, rhs=ident[:], is_transpose=True, start=(n == 0), stop=(n == len(parts) - 1)
-                )
+                start = opens and n == 0
+                stop = closes and n == len(parts) - 1
+                nc.tensor.matmul(bank[:, columns], lhsT=block, rhs=ident[:], is_transpose=True, start=start, stop=stop)
 
         def h_on_vector(s, half):
             curved, straight = products(s, half)
@@ -225,7 +229,7 @@ def tile_list_reed_register_response_kernel(
         def gather(s, piece, pieces):
             width = PICKS // pieces
             nc.vector.tensor_tensor(
-                x_sb[s][:, cols(piece, width)],
+                x_sb[s] if pieces == 1 else x_q[(s, piece)],
                 pages[s % PAGES][:].indirect(list3[:, cols(piece, width // 16)]),
                 wgt_sb[:, cols(piece, width)],
                 MULT,
@@ -274,7 +278,7 @@ def tile_list_reed_register_response_kernel(
 
         def z_parts(source, s, q):
             e = s % 2
-            return [(cols(2 * a + e, P), source[s][:, cols(2 * q + a, P)]) for a in range(2)]
+            return [(cols(2 * a + e, P), source[(s, q)][:, cols(a, P)]) for a in range(2)]
 
         def z_round(bank, rounded):
             nc.scalar.copy(
@@ -285,8 +289,9 @@ def tile_list_reed_register_response_kernel(
         def z_pair(pair, q):
             bank = next_bank()
             s0, s1 = 2 * pair, 2 * pair + 1
-            add_turned(bank, z_parts(bel_sb, s0, q) + z_parts(bel_sb, s1, q) + z_parts(x_sb, s1, q) + z_parts(x_sb, s0, q))
+            add_turned(bank, z_parts(bel_q, s0, q) + z_parts(bel_q, s1, q) + z_parts(x_q, s0, q) + z_parts(x_q, s1, q))
             z_round(bank, z_turned[pair % 2][q])
+            return bank
 
         def z_words(bank, u, rounded):
             for a in range(2):
@@ -306,11 +311,14 @@ def tile_list_reed_register_response_kernel(
             z_words(bank, 1, z_turned[1][q])
             z_weave(z0[:, cols(q, 4 * QUARTER)], bank)
         nc.vector.quantize_mx(z0_codes[:].bitcast(FP8X4), z0_sc[:], z0[:])
-        for q in range(4):
-            z_pair(2, q)
-        word_banks = [next_bank() for q in range(4)]
+        word_banks = [z_pair(2, q) for q in range(4)]
+        sum_banks = [next_bank() for q in range(4)]
+        for q in range(3):
+            add_turned(sum_banks[q], z_parts(bel_q, 6, q) + z_parts(bel_q, 7, q), closes=False)
         for q in range(4):
             z_words(word_banks[q], 0, z_turned[0][q])
+        z_last = z1[3][:, 0 : 2 * QUARTER]
+        nc.scalar.copy(z_last.rearrange("p (m u) -> p m u", u=2)[:, :, 0], word_banks[3][:, 0:QUARTER])
 
         def closing(target, t, b, q, start, stop):
             codes = z0_codes[:, cols(q, QUARTER)] if b == 0 else z1_codes[q][:]
@@ -326,37 +334,57 @@ def tile_list_reed_register_response_kernel(
                 stop=stop,
             )
 
-        sum_banks = [next_bank() for q in range(4)]
+        def open_closing(q, tiles):
+            for t in tiles:
+                bank = word_banks[q] if t == 2 else sum_banks[q]
+                closing(bank[:, cols(t % 2, QUARTER)], t, 0, q, t != 1, False)
+
+        def finish_closing(q):
+            z_quarter = z1[q][:, 0 : 2 * QUARTER].bitcast(BF16)
+            nc.vector.quantize_mx(z1_codes[q][:].bitcast(FP8X4), z1_sc[q][:], z_quarter)
+            for t in range(3):
+                bank = word_banks[q] if t == 2 else sum_banks[q]
+                closing(bank[:, cols(t % 2, QUARTER)], t, 1, q, False, t != 0)
+
+        open_closing(3, range(3))
         for q in range(4):
             gather(6, q, 4)
             gather(7, q, 4)
-            add_turned(sum_banks[q], z_parts(bel_sb, 6, q) + z_parts(bel_sb, 7, q) + z_parts(x_sb, 6, q) + z_parts(x_sb, 7, q))
+            if q < 3:
+                add_turned(sum_banks[q], z_parts(x_q, 6, q) + z_parts(x_q, 7, q), opens=False)
+        nc.vector.tensor_tensor(
+            z_last.bitcast(BF16).rearrange("p (m i) -> p m i", i=4)[:, :, 2:4],
+            turned_all[:, 4 * S : 6 * S].rearrange("p (e m) -> p m e", e=2)[:, cols(3, QUARTER), :],
+            gained_all[:, 4 * S : 6 * S].rearrange("p (e m) -> p m e", e=2)[:, cols(3, QUARTER), :],
+            ADD,
+        )
+        for q in range(3):
+            z_round(sum_banks[q], z_turned[1][q])
+            z_words(word_banks[q], 1, z_turned[1][q])
+        for q in range(3):
+            z_weave(z1[q][:, 0 : 2 * QUARTER].bitcast(BF16), word_banks[q])
+            open_closing(q, range(3))
+
         out_rows = out.rearrange("(t p) m -> p t m", p=P)
+        order = (0, 3, 1, 2)
 
-        def z_close(q):
-            two, one = sum_banks[q], word_banks[q]
-            z_quarter = z1[q][:, 0 : 2 * QUARTER].bitcast(BF16)
-            z_round(two, z_turned[1][q % 2])
-            z_words(one, 1, z_turned[1][q % 2])
-            for t in range(2):
-                closing(two[:, cols(t, QUARTER)], t, 0, q, t == 0, False)
-            z_weave(z_quarter, one)
-            closing(one[:, 0:QUARTER], 2, 0, q, True, False)
-            nc.vector.quantize_mx(z1_codes[q][:].bitcast(FP8X4), z1_sc[q][:], z_quarter)
-            for t in range(2):
-                closing(two[:, cols(t, QUARTER)], t, 1, q, False, t == 1)
-            closing(one[:, 0:QUARTER], 2, 1, q, False, True)
+        def add_bias(on_vector, y, bank, t):
+            source = bank[:, cols(t % 2, QUARTER)]
+            if on_vector:
+                nc.vector.tensor_scalar(y[:, cols(t, QUARTER)], source, bo_sb[:, t : t + 1], None, ADD)
+            else:
+                nc.scalar.activation(y[:, cols(t, QUARTER)], source, ACT.Identity, bias=bo_sb[:, t : t + 1])
 
-        def store(q):
-            two, one = sum_banks[q], word_banks[q]
-            y = z1[(q + 1) % 4]
+        def store(k):
+            q = order[k]
+            y = z1[order[(k + 1) % 4]]
             for t in range(2):
-                nc.vector.tensor_scalar(y[:, cols(t, QUARTER)], two[:, cols(t, QUARTER)], bo_sb[:, t : t + 1], None, ADD)
-            nc.scalar.activation(y[:, cols(2, QUARTER)], one[:, 0:QUARTER], ACT.Identity, bias=bo_sb[:, 2:3])
+                add_bias(k >= 2, y, sum_banks[q], t)
+            add_bias(k < 2, y, word_banks[q], 2)
             nc.sync.dma_start(out_rows[:, :, cols(q, QUARTER)], y[:].rearrange("p (t m) -> p t m", t=3))
 
-        z_close(0)
-        for q in range(4):
-            if q + 1 < 4:
-                z_close(q + 1)
-            store(q)
+        finish_closing(order[0])
+        for k in range(4):
+            if k + 1 < 4:
+                finish_closing(order[k + 1])
+            store(k)

@@ -78,7 +78,8 @@ def tile_list_reed_register_response_kernel(
         wo_codes = sb("wo_codes", 2 * N, U32)
         wo_sc = sb("wo_sc", 2 * N, U8)
         pages = [sb("page%d" % n, T2, F32) for n in range(PAGES)]
-        h_sb = [sb("h%d" % n, S, F32) for n in range(H_TILES)]
+        h_all = sb("h_all", H_TILES * S, F32)
+        h_sb = [h_all[:, cols(n, S)] for n in range(H_TILES)]
         gained_all = sb("gained_all", (SLICES - VECTOR_SLICES) * S, F32)
         gained = {s: gained_all[:, cols(s - VECTOR_SLICES, S)] for s in range(VECTOR_SLICES, SLICES)}
         turned_all = sb("turned_all", (SLICES - VECTOR_SLICES) * S, F32)
@@ -94,7 +95,7 @@ def tile_list_reed_register_response_kernel(
         z1_sc = [sb("z1_sc%d" % q, QUARTER, U8) for q in range(4)]
 
         wgs_sb = stage_a[:, 0:S]
-        wgt_sb = stage_a[:, S : 2 * S]
+        wgt_sb = stage_c[:]
         x_sb = {s: turned[s + 2] for s in range(SLICES - 2)}
         x_sb[6] = x_sb[4]
         x_sb[7] = x_sb[5]
@@ -151,17 +152,16 @@ def tile_list_reed_register_response_kernel(
 
         quantize_ws(0, stage_a[:], stage_b[:, 0 : 2 * HALF].bitcast(BF16))
         nc.sync.dma_start(wgs_sb, wgs)
-        nc.sync.dma_start(wgt_sb, wgt)
         nc.sync.dma_start(stage_b[:].rearrange("p (j c) -> p j c", j=4), ws_rows[:, :, cols(1, HALF)])
 
         for half in range(2):
             nc.vector.tensor_copy(v_codes[:, cols(half, HALF)], table[:].bitcast(U32).indirect(list1[:, cols(half, 32)]))
 
-        def products(s, half):
-            j = cols(half, HALF)
-            curved, straight = next_bank(), next_bank()
+        def products(s, j):
+            width = j.stop - j.start
+            curved, straight = next_bank()[:, 0:width], next_bank()[:, 0:width]
             nc.tensor.matmul_mx(
-                curved[:],
+                curved,
                 lhsT=wt_codes[:, cols(s, 2 * P)].bitcast(FP4X4),
                 lhsT_scale=wt_sc[:, cols(s, P)],
                 rhs=v_codes[:, j].bitcast(FP8X4),
@@ -170,7 +170,7 @@ def tile_list_reed_register_response_kernel(
                 stop=True,
             )
             nc.tensor.matmul_mx(
-                straight[:],
+                straight,
                 lhsT=ws_codes[:, cols(s, P)].bitcast(FP8X4),
                 lhsT_scale=ws_sc[:, cols(s, P)],
                 rhs=v_codes[:, j].bitcast(FP8X4),
@@ -186,20 +186,20 @@ def tile_list_reed_register_response_kernel(
                 stop = closes and n == len(parts) - 1
                 nc.tensor.matmul(bank[:, columns], lhsT=block, rhs=ident[:], is_transpose=True, start=start, stop=stop)
 
-        def h_on_vector(s, half):
-            curved, straight = products(s, half)
-            bend = stage_d[:, s * S + half * HALF : s * S + (half + 1) * HALF]
-            nc.scalar.activation(bend, curved[:], ACT.Tanh, bias=bt_sb[:, s : s + 1])
+        def h_on_vector(s, j):
+            curved, straight = products(s, j)
+            bend = (stage_c, stage_d)[s][:, j]
+            nc.scalar.activation(bend, curved, ACT.Tanh, bias=bt_sb[:, s : s + 1])
             nc.vector.scalar_tensor_tensor(
-                h_sb[s % H_TILES][:, cols(half, HALF)], bend, gain_sb[:, s : s + 1], straight[:], MULT, ADD
+                h_sb[s % H_TILES][:, j], bend, gain_sb[:, s : s + 1], straight, MULT, ADD
             )
 
         def h_front(n):
             s, half = divmod(n, 2)
-            curved, straight = products(s, half)
+            curved, straight = products(s, cols(half, HALF))
             bend = bend_st[n % STAGE_TILES]
-            nc.scalar.activation(bend[:], curved[:], ACT.Tanh, bias=bt_sb[:, s : s + 1])
-            nc.scalar.copy(straight_st[n % STAGE_TILES][:], straight[:])
+            nc.scalar.activation(bend[:], curved, ACT.Tanh, bias=bt_sb[:, s : s + 1])
+            nc.scalar.copy(straight_st[n % STAGE_TILES][:], straight)
             nc.scalar.activation(gained[s][:, cols(half, HALF)], bend[:], ACT.Copy, scale=gain_sb[:, s : s + 1])
 
         def h_middle(n):
@@ -238,14 +238,17 @@ def tile_list_reed_register_response_kernel(
         def load_bellows(s):
             nc.sync.dma_start(bel_sb[s], bel_rows[s // 4, s % 4])
 
-        h_on_vector(0, 0)
-        scatter(0, 0, 2)
-        h_on_vector(0, 1)
-        h_on_vector(1, 0)
+        h_on_vector(0, cols(0, QUARTER))
+        h_on_vector(0, cols(1, QUARTER))
+        scatter(0, 0, 4)
+        h_on_vector(0, cols(1, HALF))
+        scatter(0, 1, 4)
+        h_on_vector(1, cols(0, HALF))
         scatter(0, 1, 2)
-        h_on_vector(1, 1)
+        nc.sync.dma_start(wgt_sb, wgt)
+        quantize_ws(1, stage_b[:], h_all[:, S + HALF : 2 * S + HALF].bitcast(BF16))
+        h_on_vector(1, cols(1, HALF))
         scatter(1, 0, 1)
-        quantize_ws(1, stage_b[:], stage_c[:].bitcast(BF16))
         load_bellows(0)
         load_bellows(1)
         nc.sync.dma_start(

@@ -22,7 +22,7 @@ P = 128
 HALF = 512
 QUARTER = 256
 SLICES = 8
-VECTOR_SLICES = 2
+VECTOR_SLICES = 3
 PAGES = 3
 H_TILES = 4
 STAGE_TILES = 3
@@ -37,8 +37,8 @@ def tile_list_reed_register_response_kernel(
         keep = ctx.enter_context(tc.tile_pool(name="keep", bufs=1))
         psum = ctx.enter_context(tc.psum_pool(name="psum", bufs=1))
 
-        def sb(name, width, dtype):
-            return keep.tile([P, width], dtype, name=name, align_bytes=64)
+        def sb(name, width, dtype, tag=""):
+            return keep.tile([P, width], dtype, name=name, tag=tag, align_bytes=64)
 
         banks = [psum.tile([P, HALF], F32, name="bank%d" % n) for n in range(8)]
         turn = [0]
@@ -58,7 +58,7 @@ def tile_list_reed_register_response_kernel(
         gain_sb = sb("gain_sb", SLICES, F32)
         bo_sb = sb("bo_sb", 3, F32)
         ident = sb("ident", P, F32)
-        table = sb("table", T, I32)
+        table = sb("table", T, I32, tag="table")
         table_sc = sb("table_sc", T, U8)
         v_codes = sb("v_codes", S, U32)
         picked_sc = sb("picked_sc", S, U8)
@@ -77,7 +77,9 @@ def tile_list_reed_register_response_kernel(
         wo_bf = sb("wo_bf", 8 * N, BF16)
         wo_codes = sb("wo_codes", 2 * N, U32)
         wo_sc = sb("wo_sc", 2 * N, U8)
-        pages = [sb("page%d" % n, T2, F32) for n in range(PAGES)]
+        pages = [sb("page0", T2, F32)]
+        first_bend = sb("first_bend", QUARTER, F32, tag="first_bend")
+        stage_e = sb("stage_e", S, F32)
         h_all = sb("h_all", H_TILES * S, F32)
         h_sb = [h_all[:, cols(n, S)] for n in range(H_TILES)]
         gained_all = sb("gained_all", (SLICES - VECTOR_SLICES) * S, F32)
@@ -96,13 +98,15 @@ def tile_list_reed_register_response_kernel(
 
         wgs_sb = stage_a[:, 0:S]
         wgt_sb = stage_c[:]
-        x_sb = {s: turned[s + 2] for s in range(SLICES - 2)}
+        x_sb = {s: turned[s + 2] for s in range(1, SLICES - 2)}
+        x_sb[0] = stage_a[:, S : 2 * S]
         x_sb[6] = x_sb[4]
         x_sb[7] = x_sb[5]
         x_q = {(s, q): x_sb[s][:, cols(q, QUARTER)] for s in range(SLICES) for q in range(4)}
         bel_sb = dict(gained)
         bel_sb[0] = stage_b[:, 0:PICKS]
         bel_sb[1] = stage_b[:, PICKS : 2 * PICKS]
+        bel_sb[2] = stage_e[:]
         bel_q = {(s, q): bel_sb[s][:, cols(q, QUARTER)] for s in range(SLICES) for q in range(4)}
         bel_rows = bellows.rearrange("(b p i) m -> b i p m", b=2, i=4)
         ws_rows = ws.rearrange("(p j) c -> p j c", j=4)
@@ -138,10 +142,8 @@ def tile_list_reed_register_response_kernel(
             wt_codes[:].rearrange("p (b i q e) -> p b i q e", b=2, i=4, e=2),
             wt_raw[:].rearrange("p (b q i e) -> p b i q e", b=2, i=4, e=2),
         )
-        for page in pages:
-            engine = nc.vector if page is pages[0] else nc.gpsimd
-            for n in range(4):
-                engine.memset(page[:, cols(n, HALF)], 0.0)
+        for n in range(4):
+            nc.vector.memset(pages[0][:, cols(n, HALF)], 0.0)
 
         def quantize_ws(b, raw, rounded):
             nc.scalar.copy(
@@ -186,9 +188,8 @@ def tile_list_reed_register_response_kernel(
                 stop = closes and n == len(parts) - 1
                 nc.tensor.matmul(bank[:, columns], lhsT=block, rhs=ident[:], is_transpose=True, start=start, stop=stop)
 
-        def h_on_vector(s, j):
+        def h_on_vector(s, j, bend):
             curved, straight = products(s, j)
-            bend = (stage_c, stage_d)[s][:, j]
             nc.scalar.activation(bend, curved, ACT.Tanh, bias=bt_sb[:, s : s + 1])
             nc.vector.scalar_tensor_tensor(
                 h_sb[s % H_TILES][:, j], bend, gain_sb[:, s : s + 1], straight, MULT, ADD
@@ -238,17 +239,25 @@ def tile_list_reed_register_response_kernel(
         def load_bellows(s):
             nc.sync.dma_start(bel_sb[s], bel_rows[s // 4, s % 4])
 
-        h_on_vector(0, cols(0, QUARTER))
-        h_on_vector(0, cols(1, QUARTER))
+        h_on_vector(0, cols(0, QUARTER), first_bend[:])
+        for name, tag in (("page1", "first_bend"), ("page2", "table")):
+            pages.append(sb(name, T2, F32, tag=tag))
+            nc.gpsimd.memset(pages[-1][:], 0.0)
+        h_on_vector(0, cols(1, QUARTER), stage_c[:, cols(1, QUARTER)])
         scatter(0, 0, 4)
-        h_on_vector(0, cols(1, HALF))
+        h_on_vector(0, cols(1, HALF), stage_c[:, cols(1, HALF)])
         scatter(0, 1, 4)
-        h_on_vector(1, cols(0, HALF))
+        h_on_vector(1, cols(0, HALF), stage_d[:, cols(0, HALF)])
         scatter(0, 1, 2)
         nc.sync.dma_start(wgt_sb, wgt)
         quantize_ws(1, stage_b[:], h_all[:, S + HALF : 2 * S + HALF].bitcast(BF16))
-        h_on_vector(1, cols(1, HALF))
+        h_on_vector(1, cols(1, HALF), stage_d[:, cols(1, HALF)])
+        h_on_vector(2, cols(0, HALF), stage_e[:, cols(0, HALF)])
         scatter(1, 0, 1)
+        h_on_vector(2, cols(1, HALF), stage_e[:, cols(1, HALF)])
+        gather(0, 0, 1)
+        scatter(2, 0, 1)
+        load_bellows(2)
         load_bellows(0)
         load_bellows(1)
         nc.sync.dma_start(
@@ -357,8 +366,8 @@ def tile_list_reed_register_response_kernel(
                 add_turned(sum_banks[q], z_parts(x_q, 6, q) + z_parts(x_q, 7, q), opens=False)
         nc.vector.tensor_tensor(
             z_last.bitcast(BF16).rearrange("p (m i) -> p m i", i=4)[:, :, 2:4],
-            turned_all[:, 4 * S : 6 * S].rearrange("p (e m) -> p m e", e=2)[:, cols(3, QUARTER), :],
-            gained_all[:, 4 * S : 6 * S].rearrange("p (e m) -> p m e", e=2)[:, cols(3, QUARTER), :],
+            turned_all[:, (6 - VECTOR_SLICES) * S : (8 - VECTOR_SLICES) * S].rearrange("p (e m) -> p m e", e=2)[:, cols(3, QUARTER), :],
+            gained_all[:, (6 - VECTOR_SLICES) * S : (8 - VECTOR_SLICES) * S].rearrange("p (e m) -> p m e", e=2)[:, cols(3, QUARTER), :],
             ADD,
         )
         for q in range(3):
@@ -384,7 +393,11 @@ def tile_list_reed_register_response_kernel(
             for t in range(2):
                 add_bias(k >= 2, y, sum_banks[q], t)
             add_bias(k < 2, y, word_banks[q], 2)
-            nc.sync.dma_start(out_rows[:, :, cols(q, QUARTER)], y[:].rearrange("p (t m) -> p t m", t=3))
+            if k < 3:
+                nc.sync.dma_start(out_rows[:, :, cols(q, QUARTER)], y[:].rearrange("p (t m) -> p t m", t=3))
+            else:
+                for t in range(3):
+                    nc.sync.dma_start(out_rows[:, t, cols(q, QUARTER)], y[:, cols(t, QUARTER)])
 
         finish_closing(order[0])
         for k in range(4):

@@ -19,14 +19,18 @@ ADD = mybir.AluOpType.add
 ACT = mybir.ActivationFunctionType
 
 P = 128
+GROUP = 16
+BANKS = 8
 HALF = 512
 QUARTER = 256
 SLICES = 8
-VECTOR_SLICES = 3
+VECTOR_SLICES = 2
 PAGES = 3
 H_TILES = 4
 STAGE_TILES = 3
-LANDING = 112
+LANDING = P - 16
+LAST_PAIR = (SLICES - 2, SLICES - 1)
+DIRECT = 3
 
 
 def tile_list_reed_register_response_kernel(
@@ -40,20 +44,20 @@ def tile_list_reed_register_response_kernel(
         def sb(name, width, dtype, tag=""):
             return keep.tile([P, width], dtype, name=name, tag=tag, align_bytes=64)
 
-        banks = [psum.tile([P, HALF], F32, name="bank%d" % n) for n in range(8)]
-        turn = [0]
+        banks = [psum.tile([P, HALF], F32, name="bank%d" % n) for n in range(BANKS)]
+        uses = [0]
 
         def next_bank():
-            bank = banks[turn[0] % 8]
-            turn[0] = turn[0] + 1
+            bank = banks[uses[0] % BANKS]
+            uses[0] = uses[0] + 1
             return bank
 
         def cols(n, width):
             return slice(n * width, (n + 1) * width)
 
-        list1 = keep.tile([P, S // 16], U16, name="list1")
-        list2 = keep.tile([P, S // 16], U16, name="list2")
-        list3 = keep.tile([P, PICKS // 16], U16, name="list3")
+        list1 = keep.tile([P, S // GROUP], U16, name="list1")
+        list2 = keep.tile([P, S // GROUP], U16, name="list2")
+        list3 = keep.tile([P, PICKS // GROUP], U16, name="list3")
         bt_sb = sb("bt_sb", SLICES, F32)
         gain_sb = sb("gain_sb", SLICES, F32)
         bo_sb = sb("bo_sb", 3, F32)
@@ -79,7 +83,6 @@ def tile_list_reed_register_response_kernel(
         wo_sc = sb("wo_sc", 2 * N, U8)
         pages = [sb("page0", T2, F32)]
         first_bend = sb("first_bend", QUARTER, F32, tag="first_bend")
-        stage_e = sb("stage_e", S, F32)
         h_all = sb("h_all", H_TILES * S, F32)
         h_sb = [h_all[:, cols(n, S)] for n in range(H_TILES)]
         gained_all = sb("gained_all", (SLICES - VECTOR_SLICES) * S, F32)
@@ -98,27 +101,25 @@ def tile_list_reed_register_response_kernel(
 
         wgs_sb = stage_a[:, 0:S]
         wgt_sb = stage_c[:]
-        x_sb = {s: turned[s + 2] for s in range(1, SLICES - 2)}
-        x_sb[0] = stage_a[:, S : 2 * S]
-        x_sb[6] = x_sb[4]
-        x_sb[7] = x_sb[5]
+        x_sb = {s: turned[s + 2] for s in range(SLICES - 2)}
+        for s in LAST_PAIR:
+            x_sb[s] = x_sb[s - 2]
         x_q = {(s, q): x_sb[s][:, cols(q, QUARTER)] for s in range(SLICES) for q in range(4)}
         bel_sb = dict(gained)
-        bel_sb[0] = stage_b[:, 0:PICKS]
-        bel_sb[1] = stage_b[:, PICKS : 2 * PICKS]
-        bel_sb[2] = stage_e[:]
+        for s in range(VECTOR_SLICES):
+            bel_sb[s] = stage_b[:, cols(s, PICKS)]
         bel_q = {(s, q): bel_sb[s][:, cols(q, QUARTER)] for s in range(SLICES) for q in range(4)}
         bel_rows = bellows.rearrange("(b p i) m -> b i p m", b=2, i=4)
         ws_rows = ws.rearrange("(p j) c -> p j c", j=4)
 
         nc.sync.dma_start(list1[:], offs)
         nc.sync.dma_start(table_sc[LANDING:P, :].bitcast(I32), tab_scales[0].bitcast(I32))
+        nc.sync.dma_start(stage_a[:].rearrange("p (j c) -> p j c", j=4), ws_rows[:, :, cols(0, HALF)])
         nc.sync.dma_start(wt_sc_raw[LANDING:P, :].bitcast(I32), wt_scales[0].bitcast(I32))
         nc.sync.dma_start(wt_raw[:].bitcast(I32), wt_words[0].bitcast(I32))
+        nc.sync.dma_start(table[:], tab_words[0].rearrange("p t i -> p (t i)").bitcast(I32))
         nc.sync.dma_start(list2[:], offs2)
         nc.sync.dma_start(list3[:], offs3)
-        nc.sync.dma_start(stage_a[:].rearrange("p (j c) -> p j c", j=4), ws_rows[:, :, cols(0, HALF)])
-        nc.sync.dma_start(table[:], tab_words[0].rearrange("p t i -> p (t i)").bitcast(I32))
         nc.gpsimd.dma_start(bt_sb[:].rearrange("p (b i) -> p b i", b=2), bt.rearrange("(b p i) -> p b i", b=2, i=4))
         nc.gpsimd.dma_start(gain_sb[:].rearrange("p (b i) -> p b i", b=2), gain.rearrange("(b p i) -> p b i", b=2, i=4))
         with nc.allow_non_contiguous_dma(reason="one bias value for each partition"):
@@ -142,7 +143,7 @@ def tile_list_reed_register_response_kernel(
             wt_codes[:].rearrange("p (b i q e) -> p b i q e", b=2, i=4, e=2),
             wt_raw[:].rearrange("p (b q i e) -> p b i q e", b=2, i=4, e=2),
         )
-        for n in range(4):
+        for n in range(T2 // HALF):
             nc.vector.memset(pages[0][:, cols(n, HALF)], 0.0)
 
         def quantize_ws(b, raw, rounded):
@@ -157,7 +158,8 @@ def tile_list_reed_register_response_kernel(
         nc.sync.dma_start(stage_b[:].rearrange("p (j c) -> p j c", j=4), ws_rows[:, :, cols(1, HALF)])
 
         for half in range(2):
-            nc.vector.tensor_copy(v_codes[:, cols(half, HALF)], table[:].bitcast(U32).indirect(list1[:, cols(half, 32)]))
+            offsets = list1[:, cols(half, HALF // GROUP)]
+            nc.vector.tensor_copy(v_codes[:, cols(half, HALF)], table[:].bitcast(U32).indirect(offsets))
 
         def products(s, j):
             width = j.stop - j.start
@@ -191,11 +193,9 @@ def tile_list_reed_register_response_kernel(
         def h_on_vector(s, j, bend):
             curved, straight = products(s, j)
             nc.scalar.activation(bend, curved, ACT.Tanh, bias=bt_sb[:, s : s + 1])
-            nc.vector.scalar_tensor_tensor(
-                h_sb[s % H_TILES][:, j], bend, gain_sb[:, s : s + 1], straight, MULT, ADD
-            )
+            nc.vector.scalar_tensor_tensor(h_sb[s % H_TILES][:, j], bend, gain_sb[:, s : s + 1], straight, MULT, ADD)
 
-        def h_front(n):
+        def h_terms(n):
             s, half = divmod(n, 2)
             curved, straight = products(s, cols(half, HALF))
             bend = bend_st[n % STAGE_TILES]
@@ -203,7 +203,7 @@ def tile_list_reed_register_response_kernel(
             nc.scalar.copy(straight_st[n % STAGE_TILES][:], straight)
             nc.scalar.activation(gained[s][:, cols(half, HALF)], bend[:], ACT.Copy, scale=gain_sb[:, s : s + 1])
 
-        def h_middle(n):
+        def h_sum(n):
             s, half = divmod(n, 2)
             bank = next_bank()
             parts = [(cols(a, P), straight_st[n % STAGE_TILES][:, cols(a, P)]) for a in range(4)]
@@ -218,20 +218,18 @@ def tile_list_reed_register_response_kernel(
                 nc.tensor.transpose(bank[:, cols(a, P)], turned[s][:, cols(4 * half + a, P)], ident[:])
             nc.scalar.copy(h_sb[s % H_TILES][:, cols(half, HALF)], bank[:])
 
-        def scatter(s, piece, pieces):
-            width = S // pieces
+        def scatter(s, piece, width):
             nc.vector.tensor_tensor(
-                pages[s % PAGES][:].indirect(list2[:, cols(piece, width // 16)]),
+                pages[s % PAGES][:].indirect(list2[:, cols(piece, width // GROUP)]),
                 h_sb[s % H_TILES][:, cols(piece, width)],
                 wgs_sb[:, cols(piece, width)],
                 MULT,
             )
 
-        def gather(s, piece, pieces):
-            width = PICKS // pieces
+        def gather(s, piece, width):
             nc.vector.tensor_tensor(
-                x_sb[s] if pieces == 1 else x_q[(s, piece)],
-                pages[s % PAGES][:].indirect(list3[:, cols(piece, width // 16)]),
+                x_sb[s][:, cols(piece, width)],
+                pages[s % PAGES][:].indirect(list3[:, cols(piece, width // GROUP)]),
                 wgt_sb[:, cols(piece, width)],
                 MULT,
             )
@@ -244,53 +242,50 @@ def tile_list_reed_register_response_kernel(
             pages.append(sb(name, T2, F32, tag=tag))
             nc.gpsimd.memset(pages[-1][:], 0.0)
         h_on_vector(0, cols(1, QUARTER), stage_c[:, cols(1, QUARTER)])
-        scatter(0, 0, 4)
+        scatter(0, 0, QUARTER)
         h_on_vector(0, cols(1, HALF), stage_c[:, cols(1, HALF)])
-        scatter(0, 1, 4)
+        scatter(0, 1, QUARTER)
         h_on_vector(1, cols(0, HALF), stage_d[:, cols(0, HALF)])
-        scatter(0, 1, 2)
+        scatter(0, 1, HALF)
         nc.sync.dma_start(wgt_sb, wgt)
         quantize_ws(1, stage_b[:], h_all[:, S + HALF : 2 * S + HALF].bitcast(BF16))
         h_on_vector(1, cols(1, HALF), stage_d[:, cols(1, HALF)])
-        h_on_vector(2, cols(0, HALF), stage_e[:, cols(0, HALF)])
-        scatter(1, 0, 1)
-        h_on_vector(2, cols(1, HALF), stage_e[:, cols(1, HALF)])
-        gather(0, 0, 1)
-        scatter(2, 0, 1)
-        load_bellows(2)
-        load_bellows(0)
-        load_bellows(1)
+        scatter(1, 0, S)
+        for s in range(VECTOR_SLICES):
+            load_bellows(s)
         nc.sync.dma_start(
             stage_d[:].rearrange("p (b x) -> p b x", b=2), wo.rearrange("(b p i) n -> p b (i n)", b=2, i=4)
         )
 
         first, last = 2 * VECTOR_SLICES, 2 * SLICES - 1
-        h_front(first)
+        h_terms(first)
         for n in range(first, last + 2):
             if n + 1 <= last:
-                h_front(n + 1)
+                h_terms(n + 1)
             if n <= last:
-                h_middle(n)
+                h_sum(n)
                 if n % 2 == 1:
                     load_bellows(n // 2)
             if n - 1 >= first:
                 h_back(n - 1)
                 if (n - 1) % 2 == 1:
                     s = (n - 1) // 2
-                    gather(s - 2, 0, 1)
-                    scatter(s, 0, 1)
+                    gather(s - 2, 0, PICKS)
+                    scatter(s, 0, S)
 
         for b in range(2):
             nc.scalar.copy(
                 wo_bf[:, cols(b, 4 * N)].rearrange("p (c k i) -> p c i k", k=4, i=4),
                 stage_d[:, cols(b, 4 * N)].rearrange("p (i c k) -> p c i k", i=4, k=4),
             )
-        for lo, hi in ((0, 512), (512, 768)):
+        for lo, hi in ((0, HALF), (HALF, 2 * N)):
             nc.vector.quantize_mx(wo_codes[:, lo:hi].bitcast(FP8X4), wo_sc[:, lo:hi], wo_bf[:, 4 * lo : 4 * hi])
 
         def z_parts(source, s, q):
-            e = s % 2
-            return [(cols(2 * a + e, P), source[(s, q)][:, cols(a, P)]) for a in range(2)]
+            return [(cols(2 * a + s % 2, P), source[(s, q)][:, cols(a, P)]) for a in range(2)]
+
+        def pair_parts(source, pair, q):
+            return z_parts(source, pair[0], q) + z_parts(source, pair[1], q)
 
         def z_round(bank, rounded):
             nc.scalar.copy(
@@ -298,101 +293,104 @@ def tile_list_reed_register_response_kernel(
                 bank[:].rearrange("m (a e p) -> m a p e", a=2, e=2),
             )
 
-        def z_pair(pair, q):
+        def z_pair(g, q):
             bank = next_bank()
-            s0, s1 = 2 * pair, 2 * pair + 1
-            add_turned(bank, z_parts(bel_q, s0, q) + z_parts(bel_q, s1, q) + z_parts(x_q, s0, q) + z_parts(x_q, s1, q))
-            z_round(bank, z_turned[pair % 2][q])
+            pair = (2 * g, 2 * g + 1)
+            add_turned(bank, pair_parts(bel_q, pair, q) + pair_parts(x_q, pair, q))
+            z_round(bank, z_turned[g % 2][q])
             return bank
 
-        def z_words(bank, u, rounded):
+        def z_words(bank, u, q):
             for a in range(2):
-                nc.tensor.transpose(bank[:, cols(2 * u + a, P)], rounded[:].bitcast(F32)[:, cols(a, P)], ident[:])
+                words = z_turned[u][q][:].bitcast(F32)[:, cols(a, P)]
+                nc.tensor.transpose(bank[:, cols(2 * u + a, P)], words, ident[:])
 
-        def z_weave(z_quarter, bank):
+        def z_weave(z_words_out, bank):
             nc.scalar.copy(
-                z_quarter.bitcast(F32).rearrange("p (m u) -> p m u", u=2), bank[:].rearrange("p (u m) -> p m u", u=2)
+                z_words_out.rearrange("p (m u) -> p m u", u=2), bank[:].rearrange("p (u m) -> p m u", u=2)
             )
 
-        for pair in range(2):
+        for g in range(2):
             for q in range(4):
-                z_pair(pair, q)
+                z_pair(g, q)
         for q in range(4):
             bank = next_bank()
-            z_words(bank, 0, z_turned[0][q])
-            z_words(bank, 1, z_turned[1][q])
-            z_weave(z0[:, cols(q, 4 * QUARTER)], bank)
+            z_words(bank, 0, q)
+            z_words(bank, 1, q)
+            z_weave(z0[:, cols(q, 4 * QUARTER)].bitcast(F32), bank)
         nc.vector.quantize_mx(z0_codes[:].bitcast(FP8X4), z0_sc[:], z0[:])
+
+        turned_quarters = [q for q in range(4) if q != DIRECT]
+        z1_words = [z1[q][:, 0 : 2 * QUARTER] for q in range(4)]
         word_banks = [z_pair(2, q) for q in range(4)]
         sum_banks = [next_bank() for q in range(4)]
-        for q in range(3):
-            add_turned(sum_banks[q], z_parts(bel_q, 6, q) + z_parts(bel_q, 7, q), closes=False)
+        for q in turned_quarters:
+            add_turned(sum_banks[q], pair_parts(bel_q, LAST_PAIR, q), closes=False)
         for q in range(4):
-            z_words(word_banks[q], 0, z_turned[0][q])
-        z_last = z1[3][:, 0 : 2 * QUARTER]
-        nc.scalar.copy(z_last.rearrange("p (m u) -> p m u", u=2)[:, :, 0], word_banks[3][:, 0:QUARTER])
+            z_words(word_banks[q], 0, q)
+        nc.scalar.copy(
+            z1_words[DIRECT].rearrange("p (m u) -> p m u", u=2)[:, :, 0], word_banks[DIRECT][:, 0:QUARTER]
+        )
 
-        def closing(target, t, b, q, start, stop):
-            codes = z0_codes[:, cols(q, QUARTER)] if b == 0 else z1_codes[q][:]
-            scales = z0_sc[:, cols(q, QUARTER)] if b == 0 else z1_sc[q][:]
-            n = cols(3 * b + t, P)
-            nc.tensor.matmul_mx(
-                target,
-                lhsT=wo_codes[:, n].bitcast(FP8X4),
-                lhsT_scale=wo_sc[:, n],
-                rhs=codes.bitcast(FP8X4),
-                rhs_scale=scales,
-                start=start,
-                stop=stop,
-            )
+        def y_bank(q, t):
+            bank = word_banks[q] if t == 2 else sum_banks[q]
+            return bank[:, cols(t % 2, QUARTER)]
 
-        def open_closing(q, tiles):
-            for t in tiles:
-                bank = word_banks[q] if t == 2 else sum_banks[q]
-                closing(bank[:, cols(t % 2, QUARTER)], t, 0, q, t != 1, False)
+        def closing_pass(b, q, codes, scales):
+            for t in range(3):
+                n = cols(3 * b + t, P)
+                nc.tensor.matmul_mx(
+                    y_bank(q, t),
+                    lhsT=wo_codes[:, n].bitcast(FP8X4),
+                    lhsT_scale=wo_sc[:, n],
+                    rhs=codes.bitcast(FP8X4),
+                    rhs_scale=scales,
+                    start=(b == 0 and t != 1),
+                    stop=(b == 1 and t != 0),
+                )
+
+        def open_closing(q):
+            closing_pass(0, q, z0_codes[:, cols(q, QUARTER)], z0_sc[:, cols(q, QUARTER)])
 
         def finish_closing(q):
-            z_quarter = z1[q][:, 0 : 2 * QUARTER].bitcast(BF16)
-            nc.vector.quantize_mx(z1_codes[q][:].bitcast(FP8X4), z1_sc[q][:], z_quarter)
-            for t in range(3):
-                bank = word_banks[q] if t == 2 else sum_banks[q]
-                closing(bank[:, cols(t % 2, QUARTER)], t, 1, q, False, t != 0)
+            nc.vector.quantize_mx(z1_codes[q][:].bitcast(FP8X4), z1_sc[q][:], z1_words[q].bitcast(BF16))
+            closing_pass(1, q, z1_codes[q][:], z1_sc[q][:])
 
-        open_closing(3, range(3))
+        open_closing(DIRECT)
         for q in range(4):
-            gather(6, q, 4)
-            gather(7, q, 4)
-            if q < 3:
-                add_turned(sum_banks[q], z_parts(x_q, 6, q) + z_parts(x_q, 7, q), opens=False)
+            for s in LAST_PAIR:
+                gather(s, q, QUARTER)
+            if q != DIRECT:
+                add_turned(sum_banks[q], pair_parts(x_q, LAST_PAIR, q), opens=False)
+        last_two = slice((SLICES - VECTOR_SLICES - 2) * S, (SLICES - VECTOR_SLICES) * S)
         nc.vector.tensor_tensor(
-            z_last.bitcast(BF16).rearrange("p (m i) -> p m i", i=4)[:, :, 2:4],
-            turned_all[:, (6 - VECTOR_SLICES) * S : (8 - VECTOR_SLICES) * S].rearrange("p (e m) -> p m e", e=2)[:, cols(3, QUARTER), :],
-            gained_all[:, (6 - VECTOR_SLICES) * S : (8 - VECTOR_SLICES) * S].rearrange("p (e m) -> p m e", e=2)[:, cols(3, QUARTER), :],
+            z1_words[DIRECT].bitcast(BF16).rearrange("p (m i) -> p m i", i=4)[:, :, 2:4],
+            turned_all[:, last_two].rearrange("p (e m) -> p m e", e=2)[:, cols(DIRECT, QUARTER), :],
+            gained_all[:, last_two].rearrange("p (e m) -> p m e", e=2)[:, cols(DIRECT, QUARTER), :],
             ADD,
         )
-        for q in range(3):
+        for q in turned_quarters:
             z_round(sum_banks[q], z_turned[1][q])
-            z_words(word_banks[q], 1, z_turned[1][q])
-        for q in range(3):
-            z_weave(z1[q][:, 0 : 2 * QUARTER].bitcast(BF16), word_banks[q])
-            open_closing(q, range(3))
+            z_words(word_banks[q], 1, q)
+        for q in turned_quarters:
+            z_weave(z1_words[q], word_banks[q])
+            open_closing(q)
 
         out_rows = out.rearrange("(t p) m -> p t m", p=P)
-        order = (0, 3, 1, 2)
+        order = turned_quarters[:1] + [DIRECT] + turned_quarters[1:]
 
-        def add_bias(on_vector, y, bank, t):
-            source = bank[:, cols(t % 2, QUARTER)]
+        def add_bias(on_vector, y, q, t):
             if on_vector:
-                nc.vector.tensor_scalar(y[:, cols(t, QUARTER)], source, bo_sb[:, t : t + 1], None, ADD)
+                nc.vector.tensor_scalar(y[:, cols(t, QUARTER)], y_bank(q, t), bo_sb[:, t : t + 1], None, ADD)
             else:
-                nc.scalar.activation(y[:, cols(t, QUARTER)], source, ACT.Identity, bias=bo_sb[:, t : t + 1])
+                nc.scalar.activation(y[:, cols(t, QUARTER)], y_bank(q, t), ACT.Identity, bias=bo_sb[:, t : t + 1])
 
         def store(k):
             q = order[k]
             y = z1[order[(k + 1) % 4]]
             for t in range(2):
-                add_bias(k >= 2, y, sum_banks[q], t)
-            add_bias(k < 2, y, word_banks[q], 2)
+                add_bias(k >= 2, y, q, t)
+            add_bias(k < 2, y, q, 2)
             if k < 3:
                 nc.sync.dma_start(out_rows[:, :, cols(q, QUARTER)], y[:].rearrange("p (t m) -> p t m", t=3))
             else:

from contextlib import ExitStack

import concourse.mybir as mybir
from concourse.masks import make_identity

K, T, H, S, PICKS, T2, N = 512, 4096, 1024, 1024, 1024, 2048, 384
FLOPS = 2 * (2 * K * H * S + H * N * PICKS)

F32 = mybir.dt.float32
BF16 = mybir.dt.bfloat16
I32 = mybir.dt.int32
U32 = mybir.dt.uint32
U16 = mybir.dt.uint16
U8 = mybir.dt.uint8
FP8X4 = mybir.dt.float8_e4m3fn_x4
FP4X4 = mybir.dt.float4_e2m1fn_x4
MULT = mybir.AluOpType.mult
ADD = mybir.AluOpType.add
ACT = mybir.ActivationFunctionType

P = 128
GROUP = 16
BANKS = 8
HALF = 512
QUARTER = 256
SLICES = 8
VECTOR_SLICES = 2
PAGES = 3
H_TILES = 4
STAGE_TILES = 3
LANDING = P - 16
LAST_PAIR = (SLICES - 2, SLICES - 1)
DIRECT = 3


def tile_list_reed_register_response_kernel(
    tc, tab_words, tab_scales, offs, offs2, offs3, wt_words, wt_scales, bt, gain, ws, wgs, wgt, bellows, wo, bo, out
):
    nc = tc.nc
    with ExitStack() as ctx:
        keep = ctx.enter_context(tc.tile_pool(name="keep", bufs=1))
        psum = ctx.enter_context(tc.psum_pool(name="psum", bufs=1))

        def sb(name, width, dtype, tag=""):
            return keep.tile([P, width], dtype, name=name, tag=tag, align_bytes=64)

        banks = [psum.tile([P, HALF], F32, name="bank%d" % n) for n in range(BANKS)]
        uses = [0]

        def next_bank():
            bank = banks[uses[0] % BANKS]
            uses[0] = uses[0] + 1
            return bank

        def cols(n, width):
            return slice(n * width, (n + 1) * width)

        list1 = keep.tile([P, S // GROUP], U16, name="list1")
        list2 = keep.tile([P, S // GROUP], U16, name="list2")
        list3 = keep.tile([P, PICKS // GROUP], U16, name="list3")
        bt_sb = sb("bt_sb", SLICES, F32)
        gain_sb = sb("gain_sb", SLICES, F32)
        bo_sb = sb("bo_sb", 3, F32)
        ident = sb("ident", P, F32)
        table = sb("table", T, I32, tag="table")
        table_sc = sb("table_sc", T, U8)
        v_codes = sb("v_codes", S, U32)
        picked_sc = sb("picked_sc", S, U8)
        planes = sb("planes", S + H, U8)
        v_sc = planes[:, 0:S]
        wt_sc = planes[:, S : S + H]
        wt_raw = sb("wt_raw", 2 * H, U8)
        wt_codes = sb("wt_codes", 2 * H, U8)
        wt_sc_raw = sb("wt_sc_raw", H, U8)
        stage_a = sb("stage_a", 4 * HALF, F32)
        stage_b = sb("stage_b", 4 * HALF, F32)
        stage_c = sb("stage_c", 2 * HALF, F32)
        stage_d = sb("stage_d", 8 * N, F32)
        ws_codes = sb("ws_codes", H, U32)
        ws_sc = sb("ws_sc", H, U8)
        wo_bf = sb("wo_bf", 8 * N, BF16)
        wo_codes = sb("wo_codes", 2 * N, U32)
        wo_sc = sb("wo_sc", 2 * N, U8)
        pages = [sb("page0", T2, F32)]
        first_bend = sb("first_bend", QUARTER, F32, tag="first_bend")
        h_all = sb("h_all", H_TILES * S, F32)
        h_sb = [h_all[:, cols(n, S)] for n in range(H_TILES)]
        gained_all = sb("gained_all", (SLICES - VECTOR_SLICES) * S, F32)
        gained = {s: gained_all[:, cols(s - VECTOR_SLICES, S)] for s in range(VECTOR_SLICES, SLICES)}
        turned_all = sb("turned_all", (SLICES - VECTOR_SLICES) * S, F32)
        turned = {s: turned_all[:, cols(s - VECTOR_SLICES, S)] for s in range(VECTOR_SLICES, SLICES)}
        bend_st = [sb("bend%d" % n, HALF, F32) for n in range(STAGE_TILES)]
        straight_st = [sb("straight%d" % n, HALF, F32) for n in range(STAGE_TILES)]
        z_turned = [[sb("zt%d_%d" % (u, q), HALF, BF16) for q in range(4)] for u in range(2)]
        z0 = sb("z0", 4 * PICKS, BF16)
        z0_codes = sb("z0_codes", PICKS, U32)
        z0_sc = sb("z0_sc", PICKS, U8)
        z1 = [sb("z1_%d" % q, 3 * QUARTER, F32) for q in range(4)]
        z1_codes = [sb("z1_codes%d" % q, QUARTER, U32) for q in range(4)]
        z1_sc = [sb("z1_sc%d" % q, QUARTER, U8) for q in range(4)]

        wgs_sb = stage_a[:, 0:S]
        wgt_sb = stage_c[:]
        x_sb = {s: turned[s + 2] for s in range(SLICES - 2)}
        for s in LAST_PAIR:
            x_sb[s] = x_sb[s - 2]
        x_q = {(s, q): x_sb[s][:, cols(q, QUARTER)] for s in range(SLICES) for q in range(4)}
        bel_sb = dict(gained)
        for s in range(VECTOR_SLICES):
            bel_sb[s] = stage_b[:, cols(s, PICKS)]
        bel_q = {(s, q): bel_sb[s][:, cols(q, QUARTER)] for s in range(SLICES) for q in range(4)}
        bel_rows = bellows.rearrange("(b p i) m -> b i p m", b=2, i=4)
        ws_rows = ws.rearrange("(p j) c -> p j c", j=4)

        nc.sync.dma_start(list1[:], offs)
        nc.sync.dma_start(table_sc[LANDING:P, :].bitcast(I32), tab_scales[0].bitcast(I32))
        nc.sync.dma_start(stage_a[:].rearrange("p (j c) -> p j c", j=4), ws_rows[:, :, cols(0, HALF)])
        nc.sync.dma_start(wt_sc_raw[LANDING:P, :].bitcast(I32), wt_scales[0].bitcast(I32))
        nc.sync.dma_start(wt_raw[:].bitcast(I32), wt_words[0].bitcast(I32))
        nc.sync.dma_start(table[:], tab_words[0].rearrange("p t i -> p (t i)").bitcast(I32))
        nc.sync.dma_start(list2[:], offs2)
        nc.sync.dma_start(list3[:], offs3)
        nc.gpsimd.dma_start(bt_sb[:].rearrange("p (b i) -> p b i", b=2), bt.rearrange("(b p i) -> p b i", b=2, i=4))
        nc.gpsimd.dma_start(gain_sb[:].rearrange("p (b i) -> p b i", b=2), gain.rearrange("(b p i) -> p b i", b=2, i=4))
        with nc.allow_non_contiguous_dma(reason="one bias value for each partition"):
            nc.gpsimd.dma_start(bo_sb[:], bo.rearrange("(t p) -> p t", p=P))
        make_identity(nc, ident[:])
        nc.vector.memset(table_sc[0:LANDING, :].bitcast(I32), 0)
        nc.vector.memset(wt_sc_raw[0:LANDING, :].bitcast(I32), 0)

        nc.vector.tensor_copy(picked_sc[:], table_sc[:].indirect(list1[:]))
        nc.vector.tensor_copy(v_sc.bitcast(I32), picked_sc[:].bitcast(I32))
        nc.vector.tensor_copy(
            wt_sc.rearrange("p (b i q) -> p b i q", b=2, i=4),
            wt_sc_raw[:].rearrange("p (b q i) -> p b i q", b=2, i=4),
        )
        for quad in range(4):
            nc.sync.dma_start(
                planes[32 * quad : 32 * quad + 4, :].bitcast(I32),
                planes[LANDING + 4 * quad : LANDING + 4 * quad + 4, :].bitcast(I32),
            )
        nc.vector.tensor_copy(
            wt_codes[:].rearrange("p (b i q e) -> p b i q e", b=2, i=4, e=2),
            wt_raw[:].rearrange("p (b q i e) -> p b i q e", b=2, i=4, e=2),
        )
        for n in range(T2 // HALF):
            nc.vector.memset(pages[0][:, cols(n, HALF)], 0.0)

        def quantize_ws(b, raw, rounded):
            nc.scalar.copy(
                rounded.rearrange("p (t m j) -> p m t j", t=4, j=4),
                raw.rearrange("p (j m t) -> p m t j", j=4, t=4),
            )
            nc.vector.quantize_mx(ws_codes[:, cols(b, HALF)].bitcast(FP8X4), ws_sc[:, cols(b, HALF)], rounded)

        quantize_ws(0, stage_a[:], stage_b[:, 0 : 2 * HALF].bitcast(BF16))
        nc.sync.dma_start(wgs_sb, wgs)
        nc.sync.dma_start(stage_b[:].rearrange("p (j c) -> p j c", j=4), ws_rows[:, :, cols(1, HALF)])

        for half in range(2):
            offsets = list1[:, cols(half, HALF // GROUP)]
            nc.vector.tensor_copy(v_codes[:, cols(half, HALF)], table[:].bitcast(U32).indirect(offsets))

        def products(s, j):
            width = j.stop - j.start
            curved, straight = next_bank()[:, 0:width], next_bank()[:, 0:width]
            nc.tensor.matmul_mx(
                curved,
                lhsT=wt_codes[:, cols(s, 2 * P)].bitcast(FP4X4),
                lhsT_scale=wt_sc[:, cols(s, P)],
                rhs=v_codes[:, j].bitcast(FP8X4),
                rhs_scale=v_sc[:, j],
                start=True,
                stop=True,
            )
            nc.tensor.matmul_mx(
                straight,
                lhsT=ws_codes[:, cols(s, P)].bitcast(FP8X4),
                lhsT_scale=ws_sc[:, cols(s, P)],
                rhs=v_codes[:, j].bitcast(FP8X4),
                rhs_scale=v_sc[:, j],
                start=True,
                stop=True,
            )
            return curved, straight

        def add_turned(bank, parts, opens=True, closes=True):
            for n, (columns, block) in enumerate(parts):
                start = opens and n == 0
                stop = closes and n == len(parts) - 1
                nc.tensor.matmul(bank[:, columns], lhsT=block, rhs=ident[:], is_transpose=True, start=start, stop=stop)

        def h_on_vector(s, j, bend):
            curved, straight = products(s, j)
            nc.scalar.activation(bend, curved, ACT.Tanh, bias=bt_sb[:, s : s + 1])
            nc.vector.scalar_tensor_tensor(h_sb[s % H_TILES][:, j], bend, gain_sb[:, s : s + 1], straight, MULT, ADD)

        def h_terms(n):
            s, half = divmod(n, 2)
            curved, straight = products(s, cols(half, HALF))
            bend = bend_st[n % STAGE_TILES]
            nc.scalar.activation(bend[:], curved, ACT.Tanh, bias=bt_sb[:, s : s + 1])
            nc.scalar.copy(straight_st[n % STAGE_TILES][:], straight)
            nc.scalar.activation(gained[s][:, cols(half, HALF)], bend[:], ACT.Copy, scale=gain_sb[:, s : s + 1])

        def h_sum(n):
            s, half = divmod(n, 2)
            bank = next_bank()
            parts = [(cols(a, P), straight_st[n % STAGE_TILES][:, cols(a, P)]) for a in range(4)]
            parts = parts + [(cols(a, P), gained[s][:, cols(4 * half + a, P)]) for a in range(4)]
            add_turned(bank, parts)
            nc.scalar.copy(turned[s][:, cols(half, HALF)], bank[:])

        def h_back(n):
            s, half = divmod(n, 2)
            bank = next_bank()
            for a in range(4):
                nc.tensor.transpose(bank[:, cols(a, P)], turned[s][:, cols(4 * half + a, P)], ident[:])
            nc.scalar.copy(h_sb[s % H_TILES][:, cols(half, HALF)], bank[:])

        def scatter(s, piece, width):
            nc.vector.tensor_tensor(
                pages[s % PAGES][:].indirect(list2[:, cols(piece, width // GROUP)]),
                h_sb[s % H_TILES][:, cols(piece, width)],
                wgs_sb[:, cols(piece, width)],
                MULT,
            )

        def gather(s, piece, width):
            nc.vector.tensor_tensor(
                x_sb[s][:, cols(piece, width)],
                pages[s % PAGES][:].indirect(list3[:, cols(piece, width // GROUP)]),
                wgt_sb[:, cols(piece, width)],
                MULT,
            )

        def load_bellows(s):
            nc.sync.dma_start(bel_sb[s], bel_rows[s // 4, s % 4])

        h_on_vector(0, cols(0, QUARTER), first_bend[:])
        for name, tag in (("page1", "first_bend"), ("page2", "table")):
            pages.append(sb(name, T2, F32, tag=tag))
            nc.gpsimd.memset(pages[-1][:], 0.0)
        h_on_vector(0, cols(1, QUARTER), stage_c[:, cols(1, QUARTER)])
        scatter(0, 0, QUARTER)
        h_on_vector(0, cols(1, HALF), stage_c[:, cols(1, HALF)])
        scatter(0, 1, QUARTER)
        h_on_vector(1, cols(0, HALF), stage_d[:, cols(0, HALF)])
        scatter(0, 1, HALF)
        nc.sync.dma_start(wgt_sb, wgt)
        quantize_ws(1, stage_b[:], h_all[:, S + HALF : 2 * S + HALF].bitcast(BF16))
        h_on_vector(1, cols(1, HALF), stage_d[:, cols(1, HALF)])
        scatter(1, 0, S)
        for s in range(VECTOR_SLICES):
            load_bellows(s)
        nc.sync.dma_start(
            stage_d[:].rearrange("p (b x) -> p b x", b=2), wo.rearrange("(b p i) n -> p b (i n)", b=2, i=4)
        )

        first, last = 2 * VECTOR_SLICES, 2 * SLICES - 1
        h_terms(first)
        for n in range(first, last + 2):
            if n + 1 <= last:
                h_terms(n + 1)
            if n <= last:
                h_sum(n)
                if n % 2 == 1:
                    load_bellows(n // 2)
            if n - 1 >= first:
                h_back(n - 1)
                if (n - 1) % 2 == 1:
                    s = (n - 1) // 2
                    gather(s - 2, 0, PICKS)
                    scatter(s, 0, S)

        for b in range(2):
            nc.scalar.copy(
                wo_bf[:, cols(b, 4 * N)].rearrange("p (c k i) -> p c i k", k=4, i=4),
                stage_d[:, cols(b, 4 * N)].rearrange("p (i c k) -> p c i k", i=4, k=4),
            )
        for lo, hi in ((0, HALF), (HALF, 2 * N)):
            nc.vector.quantize_mx(wo_codes[:, lo:hi].bitcast(FP8X4), wo_sc[:, lo:hi], wo_bf[:, 4 * lo : 4 * hi])

        def z_parts(source, s, q):
            return [(cols(2 * a + s % 2, P), source[(s, q)][:, cols(a, P)]) for a in range(2)]

        def pair_parts(source, pair, q):
            return z_parts(source, pair[0], q) + z_parts(source, pair[1], q)

        def z_round(bank, rounded):
            nc.scalar.copy(
                rounded[:].rearrange("m (a p e) -> m a p e", a=2, e=2),
                bank[:].rearrange("m (a e p) -> m a p e", a=2, e=2),
            )

        def z_pair(g, q):
            bank = next_bank()
            pair = (2 * g, 2 * g + 1)
            add_turned(bank, pair_parts(bel_q, pair, q) + pair_parts(x_q, pair, q))
            z_round(bank, z_turned[g % 2][q])
            return bank

        def z_words(bank, u, q):
            for a in range(2):
                words = z_turned[u][q][:].bitcast(F32)[:, cols(a, P)]
                nc.tensor.transpose(bank[:, cols(2 * u + a, P)], words, ident[:])

        def z_weave(z_words_out, bank):
            nc.scalar.copy(
                z_words_out.rearrange("p (m u) -> p m u", u=2), bank[:].rearrange("p (u m) -> p m u", u=2)
            )

        for g in range(2):
            for q in range(4):
                z_pair(g, q)
        for q in range(4):
            bank = next_bank()
            z_words(bank, 0, q)
            z_words(bank, 1, q)
            z_weave(z0[:, cols(q, 4 * QUARTER)].bitcast(F32), bank)
        nc.vector.quantize_mx(z0_codes[:].bitcast(FP8X4), z0_sc[:], z0[:])

        turned_quarters = [q for q in range(4) if q != DIRECT]
        z1_words = [z1[q][:, 0 : 2 * QUARTER] for q in range(4)]
        word_banks = [z_pair(2, q) for q in range(4)]
        sum_banks = [next_bank() for q in range(4)]
        for q in turned_quarters:
            add_turned(sum_banks[q], pair_parts(bel_q, LAST_PAIR, q), closes=False)
        for q in range(4):
            z_words(word_banks[q], 0, q)
        nc.scalar.copy(
            z1_words[DIRECT].rearrange("p (m u) -> p m u", u=2)[:, :, 0], word_banks[DIRECT][:, 0:QUARTER]
        )

        def y_bank(q, t):
            bank = word_banks[q] if t == 2 else sum_banks[q]
            return bank[:, cols(t % 2, QUARTER)]

        def closing_pass(b, q, codes, scales):
            for t in range(3):
                n = cols(3 * b + t, P)
                nc.tensor.matmul_mx(
                    y_bank(q, t),
                    lhsT=wo_codes[:, n].bitcast(FP8X4),
                    lhsT_scale=wo_sc[:, n],
                    rhs=codes.bitcast(FP8X4),
                    rhs_scale=scales,
                    start=(b == 0 and t != 1),
                    stop=(b == 1 and t != 0),
                )

        def open_closing(q):
            closing_pass(0, q, z0_codes[:, cols(q, QUARTER)], z0_sc[:, cols(q, QUARTER)])

        def finish_closing(q):
            nc.vector.quantize_mx(z1_codes[q][:].bitcast(FP8X4), z1_sc[q][:], z1_words[q].bitcast(BF16))
            closing_pass(1, q, z1_codes[q][:], z1_sc[q][:])

        open_closing(DIRECT)
        for q in range(4):
            for s in LAST_PAIR:
                gather(s, q, QUARTER)
            if q != DIRECT:
                add_turned(sum_banks[q], pair_parts(x_q, LAST_PAIR, q), opens=False)
        last_two = slice((SLICES - VECTOR_SLICES - 2) * S, (SLICES - VECTOR_SLICES) * S)
        nc.vector.tensor_tensor(
            z1_words[DIRECT].bitcast(BF16).rearrange("p (m i) -> p m i", i=4)[:, :, 2:4],
            turned_all[:, last_two].rearrange("p (e m) -> p m e", e=2)[:, cols(DIRECT, QUARTER), :],
            gained_all[:, last_two].rearrange("p (e m) -> p m e", e=2)[:, cols(DIRECT, QUARTER), :],
            ADD,
        )
        for q in turned_quarters:
            z_round(sum_banks[q], z_turned[1][q])
            z_words(word_banks[q], 1, q)
        for q in turned_quarters:
            z_weave(z1_words[q], word_banks[q])
            open_closing(q)

        out_rows = out.rearrange("(t p) m -> p t m", p=P)
        order = turned_quarters[:1] + [DIRECT] + turned_quarters[1:]

        def add_bias(on_vector, y, q, t):
            if on_vector:
                nc.vector.tensor_scalar(y[:, cols(t, QUARTER)], y_bank(q, t), bo_sb[:, t : t + 1], None, ADD)
            else:
                nc.scalar.activation(y[:, cols(t, QUARTER)], y_bank(q, t), ACT.Identity, bias=bo_sb[:, t : t + 1])

        def store(k):
            q = order[k]
            y = z1[order[(k + 1) % 4]]
            for t in range(2):
                add_bias(k >= 2, y, q, t)
            add_bias(k < 2, y, q, 2)
            if k < 3:
                nc.sync.dma_start(out_rows[:, :, cols(q, QUARTER)], y[:].rearrange("p (t m) -> p t m", t=3))
            else:
                for t in range(3):
                    nc.sync.dma_start(out_rows[:, t, cols(q, QUARTER)], y[:, cols(t, QUARTER)])

        finish_closing(order[0])
        for k in range(4):
            if k + 1 < 4:
                finish_closing(order[k + 1])
            store(k)
